import numpy as np
import ml_dtypes


def mxq(x, axis, fmt="e4m3"):
    dtype, down = {"e4m3": (ml_dtypes.float8_e4m3fn, 7), "e5m2": (ml_dtypes.float8_e5m2, 14)}[fmt]
    v = np.moveaxis(np.asarray(x, np.float32).astype(ml_dtypes.bfloat16).astype(np.float64), axis, -1)
    blocks = v.reshape(v.shape[:-1] + (-1, 32))
    amax = np.abs(blocks).max(-1, keepdims=True)
    byte = np.maximum(np.where(amax > 0, np.frexp(amax)[1] - 1 + 127, 0) - down, 1)
    scale = np.exp2(byte - 127.0)
    codes = (blocks / scale).astype(np.float32).astype(dtype).astype(np.float64)
    return np.moveaxis((codes * scale).reshape(v.shape), -1, axis)


WIDE = False


def mx_kscale(k):
    if not WIDE:
        return np.ones(k)
    levels = np.array([10, -10, 5, -5, 0])
    if k % 512:
        return np.exp2(np.random.permutation(np.resize(levels, k // 32))).repeat(32)
    a = np.empty((k // 512, 16))
    for p in range(k // 512):
        a[p, :8] = np.random.permutation(np.resize(levels, 8))
        for g in range(8):
            far = levels[np.abs(levels - a[p, g]) >= 10]
            a[p, g + 8] = far[np.random.randint(len(far))]
    return np.exp2(a.ravel()).repeat(32)


def f64(x):
    return np.asarray(x).astype(np.float64)


def striped(idx):
    return np.tile(idx.reshape(-1, 16).T, (8, 1)).astype(np.uint16)


def unstriped(offs):
    return offs[:16].T.reshape(-1).astype(np.int64)


def pack_weight(w):
    k, n = w.shape
    w = f64(np.asarray(w, np.float32).astype(ml_dtypes.bfloat16)).reshape(k // 32, 32, n)
    amax = np.abs(w).max(1)
    byte = np.clip(np.where(amax > 0, np.frexp(amax)[1] - 1 + 127 - 7, 1), 1, 254)
    scaled = (w * np.exp2(127.0 - byte)[:, None, :]).reshape(k, n).astype(np.float32)
    words = np.ascontiguousarray(scaled.reshape(k // 512, 128, 4, n).transpose(0, 1, 3, 2)).astype(ml_dtypes.float8_e4m3fn).view(np.uint8)
    return words, np.ascontiguousarray(byte.astype(np.uint8).reshape(k // 512, 16, n))


def unpack_weight(words, scales):
    g, p, n, _ = words.shape
    vals = np.ascontiguousarray(words).view(ml_dtypes.float8_e4m3fn).astype(np.float64) * np.repeat(np.exp2(scales.astype(np.float64) - 127.0), 8, axis=1)[..., None]
    return vals.transpose(0, 1, 3, 2).reshape(g * 512, n)


def sigmoid(v):
    return 1.0 / (1.0 + np.exp(-np.maximum(v, -700.0)))


K, T, S, N, H, W, U = 512, 2048, 512, 512, 512, 384, 256


def setup_inputs():
    n = np.random.standard_normal
    s = mx_kscale(K)[:, None]
    u = mx_kscale(H)
    packed_xT = pack_weight(n((K, T)) * s)
    perm = np.random.permutation(S)
    return {
        "x_words": packed_xT[0],
        "x_scales": packed_xT[1],
        "w1": (n((K, H)) / np.sqrt(K) / s).astype(np.float32),
        "gn": (np.random.uniform(0.5, 1.5, (H, 1)) * u[:, None]).astype(np.float32),
        "w2": (n((H, N)) / np.sqrt(2 * H) / u[:, None]).astype(np.float32),
        "w3": (n((K, N)) / np.sqrt(2 * K) / s).astype(np.float32),
        "offs": striped(np.random.permutation(T)[:S]),
        "n1": striped(np.random.permutation(S)[:W]),
        "n2": striped(np.random.permutation(S)[:W]),
        "two": striped(np.random.permutation(T)[:S]),
        "n3": striped(perm[:U]),
        "n4": striped(perm[U:]),
    }


def reference(x_words, x_scales, w1, gn, w2, w3, offs, n1, n2, two, n3, n4):
    xq = unpack_weight(x_words, x_scales)[:, unstriped(offs)]
    y = mxq(f64(w1), 0, "e4m3").T @ xq
    old = y[:, unstriped(n1)]
    pa = y[:, unstriped(n2)]
    ra = old * sigmoid(pa)
    ds = y.copy()
    ds[:, unstriped(n1)] = ra
    z = f64(gn) * ds
    x_two = unpack_weight(x_words, x_scales)[:, unstriped(two)]
    h = mxq(f64(w2), 0, "e4m3").T @ mxq(z, 0, "e4m3") + mxq(f64(w3), 0, "e4m3").T @ x_two
    pa2 = h[:, unstriped(n3)]
    pb = h[:, unstriped(n4)]
    rb = np.maximum(0.5 * pa2, pb)
    ra2 = pb - pa2
    ds2 = np.zeros((N, S))
    ds2[:, unstriped(n3)] = ra2
    out = ds2.copy()
    out[:, unstriped(n4)] = rb
    return out

@@ -1,0 +1,198 @@
+from contextlib import ExitStack
+
+import concourse.mybir as mybir
+
+K, T, S, N, H, W, U = 512, 2048, 512, 512, 512, 384, 256
+FLOPS = 2 * K * H * S + 2 * H * N * S + 2 * K * N * S
+
+F32 = mybir.dt.float32
+BF16 = mybir.dt.bfloat16
+I32 = mybir.dt.int32
+U32 = mybir.dt.uint32
+U16 = mybir.dt.uint16
+U8 = mybir.dt.uint8
+FP8X4 = mybir.dt.float8_e4m3fn_x4
+ALU = mybir.AluOpType
+ACT = mybir.ActivationFunctionType
+
+P = 128
+PACK = 4
+QUARTERS = 4
+
+
+def tile_picked_mixinkgatelift_none_p_kernel(tc, x_words, x_scales, w1, gn, w2, w3, offs, n1, n2, two, n3, n4, out):
+    nc = tc.nc
+    with ExitStack() as ctx:
+        keep = ctx.enter_context(tc.tile_pool(name="keep", bufs=1))
+        psum = ctx.enter_context(tc.psum_pool(name="psum", bufs=1))
+
+        def load_list(src, name):
+            dst = keep.tile(list(src.shape), U16, name=name)
+            nc.sync.dma_start(dst[:], src)
+            return dst
+
+        table_scales = keep.tile([P, T], U8, name="table_scales")
+        nc.vector.memset(table_scales[:].bitcast(I32), 0)
+        offs_sb = load_list(offs, "offs_sb")
+        two_sb = load_list(two, "two_sb")
+        for q in range(4):
+            nc.sync.dma_start(table_scales[32 * q : 32 * q + 4, :].bitcast(I32), x_scales[0, 4 * q : 4 * q + 4, :].bitcast(I32))
+        table_words = keep.tile([P, T], I32, name="table_words")
+        nc.sync.dma_start(table_words[:], x_words[0].rearrange("p c r -> p (c r)").bitcast(I32))
+        w1_rows = w1.rearrange("(p j) c -> p j c", j=PACK)
+        w1_raw = []
+        for c in range(QUARTERS):
+            part = keep.tile([P, PACK, P], F32, name="w1_raw%d" % c)
+            nc.sync.dma_start(part[:], w1_rows[:, :, P * c : P * (c + 1)])
+            w1_raw.append(part)
+        n2_sb = load_list(n2, "n2_sb")
+        n1_sb = load_list(n1, "n1_sb")
+        w3_rows = w3.rearrange("(p j) m -> p j m", j=PACK)
+        w3_raw = []
+        for half in range(2):
+            part = keep.tile([P, PACK, N // 2], F32, name="w3_raw%d" % half, tag="old%d" % half, align_bytes=64)
+            nc.sync.dma_start(part[:], w3_rows[:, :, 256 * half : 256 * (half + 1)])
+            w3_raw.append(part)
+        w2_raw = keep.tile([P, PACK, N], F32, name="w2_raw")
+        w2_rows = w2.rearrange("(b t e) m -> t b e m", t=PACK, e=8)
+        for t in range(PACK):
+            nc.sync.dma_start(w2_raw[:, t, :], w2_rows[t])
+        gain_rows = gn.rearrange("(b t e) o -> t b e o", t=PACK, e=8)
+        gain = [keep.tile([P, 1], F32, name="gain%d" % t) for t in range(PACK)]
+        for t in range(PACK):
+            nc.sync.dma_start(gain[t][:], gain_rows[t])
+        n3_sb = load_list(n3, "n3_sb")
+        n4_sb = load_list(n4, "n4_sb")
+
+        def mx_tiles(name, width):
+            return (keep.tile([P, width], U32, name=name + "_words", align_bytes=64),
+                    keep.tile([P, width], U8, name=name + "_scales", align_bytes=64))
+
+        xa_words, xa_scales = mx_tiles("xa", S)
+        xb_scales = keep.tile([P, S], U8, name="xb_scales", align_bytes=64)
+        nc.vector.tensor_copy(xa_scales[:], table_scales[:].indirect(offs_sb[:]))
+        nc.vector.tensor_copy(xb_scales[:], table_scales[:].indirect(two_sb[:]))
+        nc.vector.tensor_copy(xa_words[:], table_words[:].bitcast(U32).indirect(offs_sb[:]))
+
+        w1_bf = keep.tile([P, PACK, 16, 8, PACK], BF16, name="w1_bf", tag="w1_bf_then_xb", align_bytes=64)
+        for c in range(QUARTERS):
+            dst = w1_bf[:, :, 4 * c : 4 * c + 4, :, :].rearrange("p t b e j -> p b t e j")
+            src = w1_raw[c][:].rearrange("p j (b t e) -> p b t e j", t=PACK, e=8)
+            if c < QUARTERS - 1:
+                nc.scalar.copy(dst, src)
+            else:
+                nc.vector.tensor_copy(dst, src)
+        w1_words, w1_scales = mx_tiles("w1", H)
+        y_ps = []
+        for t in range(PACK):
+            cols = slice(P * t, P * (t + 1))
+            nc.vector.quantize_mx(w1_words[:, cols].bitcast(FP8X4), w1_scales[:, cols],
+                                  w1_bf[:, t].rearrange("p b e j -> p (b e j)"))
+            bank = psum.tile([P, S], F32, name="y_ps%d" % t)
+            nc.tensor.matmul_mx(bank[:], w1_words[:, cols].bitcast(FP8X4), w1_scales[:, cols],
+                                xa_words[:].bitcast(FP8X4), xa_scales[:], start=True, stop=True)
+            y_ps.append(bank)
+
+        xb_words = keep.tile([P, S], U32, name="xb_words", tag="w1_bf_then_xb", align_bytes=64)
+        nc.vector.tensor_copy(xb_words[:], table_words[:].bitcast(U32).indirect(two_sb[:]))
+
+        y = [keep.tile([P, S], F32, name="y%d" % t) for t in range(PACK)]
+        gate = [keep.tile([P, W], F32, name="gate%d" % t) for t in range(PACK)]
+        old = [keep.tile([P, W], F32, name="old%d" % t, tag="old%d" % t, align_bytes=64) for t in range(PACK)]
+        z_bf = keep.tile([P, S, PACK], BF16, name="z_bf", tag="z_bf_then_w2", align_bytes=64)
+
+        def gates(t):
+            for half in range(2):
+                nc.scalar.activation(gate[t][:, 192 * half : 192 * (half + 1)],
+                                     y[t][:].indirect(n2_sb[:, 12 * half : 12 * (half + 1)]), ACT.Sigmoid)
+
+        def make_z(t):
+            nc.vector.tensor_scalar(z_bf[:, :, t], y[t][:], gain[t][:], None, ALU.mult)
+
+        def interleave(copy, dst, src):
+            copy(dst.rearrange("p (c i) j -> p c j i", i=4), src.rearrange("p j (c i) -> p c j i", i=4))
+
+        def quantise(name, src):
+            words, scales = mx_tiles(name, N)
+            nc.vector.quantize_mx(words[:].bitcast(FP8X4), scales[:], src[:].rearrange("p m j -> p (m j)"))
+            return words, scales
+
+        w3_bf = keep.tile([P, N, PACK], BF16, name="w3_bf", align_bytes=64)
+        for half in range(2):
+            interleave(nc.vector.tensor_copy, w3_bf[:, 256 * half : 256 * (half + 1), :], w3_raw[half][:])
+        w3_words, w3_scales = quantise("w3", w3_bf)
+        h_ps = []
+        for u in range(4):
+            cols = slice(P * u, P * (u + 1))
+            bank = psum.tile([P, S], F32, name="h_ps%d" % u)
+            nc.tensor.matmul_mx(bank[:], w3_words[:, cols].bitcast(FP8X4), w3_scales[:, cols],
+                                xb_words[:].bitcast(FP8X4), xb_scales[:], start=True, stop=False)
+            h_ps.append(bank)
+
+        for t in range(PACK):
+            nc.scalar.copy(y[t][:], y_ps[t][:])
+            gates(t)
+            if t < 2:
+                nc.vector.tensor_tensor(old[t][:], y[t][:].indirect(n1_sb[:]), gate[t][:], ALU.mult)
+            else:
+                nc.scalar.activation(old[t][:], y[t][:].indirect(n1_sb[:]), ACT.Copy)
+                nc.vector.tensor_tensor(y[t][:].indirect(n1_sb[:]), old[t][:], gate[t][:], ALU.mult)
+        for t in (0, 1):
+            nc.scalar.activation(y[t][:].indirect(n1_sb[:]), old[t][:], ACT.Copy)
+        for t in (2, 3, 0, 1):
+            make_z(t)
+
+        w2_bf = keep.tile([P, N, PACK], BF16, name="w2_bf", tag="old1", align_bytes=64)
+        for u in range(4):
+            cols = slice(P * u, P * (u + 1))
+            interleave(nc.scalar.copy, w2_bf[:, cols, :], w2_raw[:, :, cols])
+        z_words, z_scales = quantise("z", z_bf)
+        w2_words = keep.tile([P, N], U32, name="w2_words", tag="z_bf_then_w2", align_bytes=64)
+        w2_scales = keep.tile([P, N], U8, name="w2_scales", align_bytes=64)
+        for u in range(4):
+            cols = slice(P * u, P * (u + 1))
+            nc.vector.quantize_mx(w2_words[:, cols].bitcast(FP8X4), w2_scales[:, cols],
+                                  w2_bf[:, cols, :].rearrange("p m j -> p (m j)"))
+            nc.tensor.matmul_mx(h_ps[u][:], w2_words[:, cols].bitcast(FP8X4), w2_scales[:, cols],
+                                z_words[:].bitcast(FP8X4), z_scales[:], start=False, stop=True)
+
+        h = [keep.tile([P, S], F32, name="h%d" % u) for u in range(4)]
+        minus_pa = [keep.tile([P, U], F32, name="minus_pa%d" % u) for u in range(4)]
+        pb = [keep.tile([P, U], F32, name="pb%d" % u) for u in range(4)]
+        rb = [keep.tile([P, U], F32, name="rb%d" % u) for u in range(4)]
+        res = [keep.tile([P, S], F32, name="res%d" % u) for u in range(4)]
+
+        def fetch_pa(u):
+            nc.scalar.activation(minus_pa[u][:], h[u][:].indirect(n3_sb[:]), ACT.Copy, scale=-1.0)
+
+        def fetch_pb(u):
+            if u == 3:
+                nc.scalar.activation(pb[u][:], h[u][:].indirect(n4_sb[:]), ACT.Copy)
+            else:
+                nc.vector.tensor_copy(pb[u][:], h[u][:].indirect(n4_sb[:]))
+
+        def larger(u):
+            nc.vector.scalar_tensor_tensor(rb[u][:], minus_pa[u][:], -0.5, pb[u][:], ALU.mult, ALU.max)
+
+        def put_difference(u):
+            nc.vector.tensor_tensor(res[u][:].indirect(n3_sb[:]), pb[u][:], minus_pa[u][:], ALU.add)
+
+        def put_larger(u):
+            nc.scalar.activation(res[u][:].indirect(n4_sb[:]), rb[u][:], ACT.Copy)
+
+        def store(u, queue):
+            queue.dma_start(out[P * u : P * (u + 1), :], res[u][:])
+
+        for u in range(4):
+            (nc.vector.tensor_copy if u % 2 else nc.scalar.copy)(h[u][:], h_ps[u][:])
+        for u in range(4):
+            fetch_pa(u)
+            fetch_pb(u)
+            larger(u)
+        for u in (0, 2):
+            put_difference(u)
+            put_larger(u + 1)
+            put_larger(u)
+            put_difference(u + 1)
+            store(u, nc.sync if u == 0 else nc.scalar)
+            store(u + 1, nc.sync)

@@ -31,6 +31,11 @@ def tile_picked_mixinkgatelift_none_p_kernel(tc, x_words, x_scales, w1, gn, w2, 
             nc.sync.dma_start(dst[:], src)
             return dst
 
+        warm_in = keep.tile([P, 1], F32, name="warm_in")
+        warm_out = keep.tile([P, 1], F32, name="warm_out")
+        nc.gpsimd.memset(warm_in[:], 0.0)
+        nc.scalar.activation(warm_out[:], warm_in[:], ACT.Sigmoid)
+
         table_scales = keep.tile([P, T], U8, name="table_scales")
         nc.vector.memset(table_scales[:].bitcast(I32), 0)
         offs_sb = load_list(offs, "offs_sb")
@@ -39,18 +44,14 @@ def tile_picked_mixinkgatelift_none_p_kernel(tc, x_words, x_scales, w1, gn, w2, 
             nc.sync.dma_start(table_scales[32 * q : 32 * q + 4, :].bitcast(I32), x_scales[0, 4 * q : 4 * q + 4, :].bitcast(I32))
         table_words = keep.tile([P, T], I32, name="table_words")
         nc.sync.dma_start(table_words[:], x_words[0].rearrange("p c r -> p (c r)").bitcast(I32))
-        w1_rows = w1.rearrange("(p j) c -> p j c", j=PACK)
-        w1_raw = []
-        for c in range(QUARTERS):
-            part = keep.tile([P, PACK, P], F32, name="w1_raw%d" % c)
-            nc.sync.dma_start(part[:], w1_rows[:, :, P * c : P * (c + 1)])
-            w1_raw.append(part)
+        w1_raw = keep.tile([P, PACK, H], F32, name="w1_raw")
+        nc.sync.dma_start(w1_raw[:], w1.rearrange("(p j) c -> p j c", j=PACK))
         n2_sb = load_list(n2, "n2_sb")
         n1_sb = load_list(n1, "n1_sb")
         w3_rows = w3.rearrange("(p j) m -> p j m", j=PACK)
         w3_raw = []
         for half in range(2):
-            part = keep.tile([P, PACK, N // 2], F32, name="w3_raw%d" % half, tag="old%d" % half, align_bytes=64)
+            part = keep.tile([P, PACK, N // 2], F32, name="w3_raw%d" % half, tag="slot%d" % half, align_bytes=64)
             nc.sync.dma_start(part[:], w3_rows[:, :, 256 * half : 256 * (half + 1)])
             w3_raw.append(part)
         w2_raw = keep.tile([P, PACK, N], F32, name="w2_raw")
@@ -75,13 +76,10 @@ def tile_picked_mixinkgatelift_none_p_kernel(tc, x_words, x_scales, w1, gn, w2, 
         nc.vector.tensor_copy(xa_words[:], table_words[:].bitcast(U32).indirect(offs_sb[:]))
 
         w1_bf = keep.tile([P, PACK, 16, 8, PACK], BF16, name="w1_bf", tag="w1_bf_then_xb", align_bytes=64)
-        for c in range(QUARTERS):
-            dst = w1_bf[:, :, 4 * c : 4 * c + 4, :, :].rearrange("p t b e j -> p b t e j")
-            src = w1_raw[c][:].rearrange("p j (b t e) -> p b t e j", t=PACK, e=8)
-            if c < QUARTERS - 1:
-                nc.scalar.copy(dst, src)
-            else:
-                nc.vector.tensor_copy(dst, src)
+        dst = w1_bf[:].rearrange("p t b e j -> p b t e j")
+        src = w1_raw[:].rearrange("p j (b t e) -> p b t e j", t=PACK, e=8)
+        nc.scalar.copy(dst[:, :6], src[:, :6])
+        nc.vector.tensor_copy(dst[:, 6:], src[:, 6:])
         w1_words, w1_scales = mx_tiles("w1", H)
         y_ps = []
         for t in range(PACK):
@@ -98,7 +96,6 @@ def tile_picked_mixinkgatelift_none_p_kernel(tc, x_words, x_scales, w1, gn, w2, 
 
         y = [keep.tile([P, S], F32, name="y%d" % t) for t in range(PACK)]
         gate = [keep.tile([P, W], F32, name="gate%d" % t) for t in range(PACK)]
-        old = [keep.tile([P, W], F32, name="old%d" % t, tag="old%d" % t, align_bytes=64) for t in range(PACK)]
         z_bf = keep.tile([P, S, PACK], BF16, name="z_bf", tag="z_bf_then_w2", align_bytes=64)
 
         def gates(t):
@@ -106,8 +103,8 @@ def tile_picked_mixinkgatelift_none_p_kernel(tc, x_words, x_scales, w1, gn, w2, 
                 nc.scalar.activation(gate[t][:, 192 * half : 192 * (half + 1)],
                                      y[t][:].indirect(n2_sb[:, 12 * half : 12 * (half + 1)]), ACT.Sigmoid)
 
-        def make_z(t):
-            nc.vector.tensor_scalar(z_bf[:, :, t], y[t][:], gain[t][:], None, ALU.mult)
+        def make_z(t, cols):
+            nc.vector.tensor_scalar(z_bf[:, cols, t], y[t][:, cols], gain[t][:], None, ALU.mult)
 
         def interleave(copy, dst, src):
             copy(dst.rearrange("p (c i) j -> p c j i", i=4), src.rearrange("p j (c i) -> p c j i", i=4))
@@ -129,32 +126,43 @@ def tile_picked_mixinkgatelift_none_p_kernel(tc, x_words, x_scales, w1, gn, w2, 
                                 xb_words[:].bitcast(FP8X4), xb_scales[:], start=True, stop=False)
             h_ps.append(bank)
 
+        ra = [keep.tile([P, W], F32, name="ra%d" % t, tag="slot%d" % t, align_bytes=64) for t in range(2)]
+        old = keep.tile([P, 2, W], F32, name="old")
         for t in range(PACK):
             nc.scalar.copy(y[t][:], y_ps[t][:])
             gates(t)
             if t < 2:
-                nc.vector.tensor_tensor(old[t][:], y[t][:].indirect(n1_sb[:]), gate[t][:], ALU.mult)
+                nc.vector.tensor_tensor(ra[t][:], y[t][:].indirect(n1_sb[:]), gate[t][:], ALU.mult)
             else:
-                nc.scalar.activation(old[t][:], y[t][:].indirect(n1_sb[:]), ACT.Copy)
-                nc.vector.tensor_tensor(y[t][:].indirect(n1_sb[:]), old[t][:], gate[t][:], ALU.mult)
+                nc.scalar.activation(old[:, t - 2, :], y[t][:].indirect(n1_sb[:]), ACT.Copy)
+                nc.vector.tensor_tensor(y[t][:].indirect(n1_sb[:]), old[:, t - 2, :], gate[t][:], ALU.mult)
         for t in (0, 1):
-            nc.scalar.activation(y[t][:].indirect(n1_sb[:]), old[t][:], ACT.Copy)
-        for t in (2, 3, 0, 1):
-            make_z(t)
+            nc.scalar.activation(y[t][:].indirect(n1_sb[:]), ra[t][:], ACT.Copy)
+        for t in (2, 3, 0):
+            make_z(t, slice(0, S))
+        halves = [slice(0, S // 2), slice(S // 2, S)]
+        for cols in halves:
+            make_z(1, cols)
 
-        w2_bf = keep.tile([P, N, PACK], BF16, name="w2_bf", tag="old1", align_bytes=64)
+        w2_bf = keep.tile([P, N, PACK], BF16, name="w2_bf", tag="slot1", align_bytes=64)
         for u in range(4):
             cols = slice(P * u, P * (u + 1))
             interleave(nc.scalar.copy, w2_bf[:, cols, :], w2_raw[:, :, cols])
-        z_words, z_scales = quantise("z", z_bf)
-        w2_words = keep.tile([P, N], U32, name="w2_words", tag="z_bf_then_w2", align_bytes=64)
+        z_words, z_scales = mx_tiles("z", S)
+        for cols in halves:
+            nc.vector.quantize_mx(z_words[:, cols].bitcast(FP8X4), z_scales[:, cols],
+                                  z_bf[:, cols, :].rearrange("p s t -> p (s t)"))
+        w2_first = keep.tile([P, P], U32, name="w2_first", align_bytes=64)
+        w2_rest = keep.tile([P, 3, P], U32, name="w2_rest", tag="z_bf_then_w2", align_bytes=64)
         w2_scales = keep.tile([P, N], U8, name="w2_scales", align_bytes=64)
         for u in range(4):
             cols = slice(P * u, P * (u + 1))
-            nc.vector.quantize_mx(w2_words[:, cols].bitcast(FP8X4), w2_scales[:, cols],
+            words = w2_first[:] if u == 0 else w2_rest[:, u - 1, :]
+            nc.vector.quantize_mx(words.bitcast(FP8X4), w2_scales[:, cols],
                                   w2_bf[:, cols, :].rearrange("p m j -> p (m j)"))
-            nc.tensor.matmul_mx(h_ps[u][:], w2_words[:, cols].bitcast(FP8X4), w2_scales[:, cols],
-                                z_words[:].bitcast(FP8X4), z_scales[:], start=False, stop=True)
+            for part in (halves if u == 0 else [slice(0, S)]):
+                nc.tensor.matmul_mx(h_ps[u][:, part], words.bitcast(FP8X4), w2_scales[:, cols],
+                                    z_words[:, part].bitcast(FP8X4), z_scales[:, part], start=False, stop=part.stop == S)
 
         h = [keep.tile([P, S], F32, name="h%d" % u) for u in range(4)]
         minus_pa = [keep.tile([P, U], F32, name="minus_pa%d" % u) for u in range(4)]

@@ -42,10 +42,10 @@ def tile_picked_mixinkgatelift_none_p_kernel(tc, x_words, x_scales, w1, gn, w2, 
         two_sb = load_list(two, "two_sb")
         for q in range(4):
             nc.sync.dma_start(table_scales[32 * q : 32 * q + 4, :].bitcast(I32), x_scales[0, 4 * q : 4 * q + 4, :].bitcast(I32))
-        table_words = keep.tile([P, T], I32, name="table_words")
-        nc.sync.dma_start(table_words[:], x_words[0].rearrange("p c r -> p (c r)").bitcast(I32))
         w1_raw = keep.tile([P, PACK, H], F32, name="w1_raw")
         nc.sync.dma_start(w1_raw[:], w1.rearrange("(p j) c -> p j c", j=PACK))
+        table_words = keep.tile([P, T], I32, name="table_words")
+        nc.sync.dma_start(table_words[:], x_words[0].rearrange("p c r -> p (c r)").bitcast(I32))
         n2_sb = load_list(n2, "n2_sb")
         n1_sb = load_list(n1, "n1_sb")
         w3_rows = w3.rearrange("(p j) m -> p j m", j=PACK)
@@ -70,41 +70,43 @@ def tile_picked_mixinkgatelift_none_p_kernel(tc, x_words, x_scales, w1, gn, w2, 
                     keep.tile([P, width], U8, name=name + "_scales", align_bytes=64))
 
         xa_words, xa_scales = mx_tiles("xa", S)
-        xb_scales = keep.tile([P, S], U8, name="xb_scales", align_bytes=64)
+        xb_words, xb_scales = mx_tiles("xb", S)
+        halves = [slice(0, S // 2), slice(S // 2, S)]
         nc.vector.tensor_copy(xa_scales[:], table_scales[:].indirect(offs_sb[:]))
         nc.vector.tensor_copy(xb_scales[:], table_scales[:].indirect(two_sb[:]))
-        nc.vector.tensor_copy(xa_words[:], table_words[:].bitcast(U32).indirect(offs_sb[:]))
 
-        w1_bf = keep.tile([P, PACK, 16, 8, PACK], BF16, name="w1_bf", tag="w1_bf_then_xb", align_bytes=64)
+        w1_bf = keep.tile([P, PACK, 16, 8, PACK], BF16, name="w1_bf", align_bytes=64)
         dst = w1_bf[:].rearrange("p t b e j -> p b t e j")
         src = w1_raw[:].rearrange("p j (b t e) -> p b t e j", t=PACK, e=8)
         nc.scalar.copy(dst[:, :6], src[:, :6])
         nc.vector.tensor_copy(dst[:, 6:], src[:, 6:])
         w1_words, w1_scales = mx_tiles("w1", H)
+        nc.vector.quantize_mx(w1_words[:].bitcast(FP8X4), w1_scales[:], w1_bf[:].rearrange("p t b e j -> p (t b e j)"))
+        for half in range(2):
+            nc.vector.tensor_copy(xa_words[:, halves[half]],
+                                  table_words[:].bitcast(U32).indirect(offs_sb[:, 16 * half : 16 * (half + 1)]))
+        nc.vector.tensor_copy(xb_words[:], table_words[:].bitcast(U32).indirect(two_sb[:]))
         y_ps = []
         for t in range(PACK):
             cols = slice(P * t, P * (t + 1))
-            nc.vector.quantize_mx(w1_words[:, cols].bitcast(FP8X4), w1_scales[:, cols],
-                                  w1_bf[:, t].rearrange("p b e j -> p (b e j)"))
             bank = psum.tile([P, S], F32, name="y_ps%d" % t)
-            nc.tensor.matmul_mx(bank[:], w1_words[:, cols].bitcast(FP8X4), w1_scales[:, cols],
-                                xa_words[:].bitcast(FP8X4), xa_scales[:], start=True, stop=True)
+            for part in halves:
+                nc.tensor.matmul_mx(bank[:, part], w1_words[:, cols].bitcast(FP8X4), w1_scales[:, cols],
+                                    xa_words[:, part].bitcast(FP8X4), xa_scales[:, part], start=True, stop=True)
             y_ps.append(bank)
-
-        xb_words = keep.tile([P, S], U32, name="xb_words", tag="w1_bf_then_xb", align_bytes=64)
-        nc.vector.tensor_copy(xb_words[:], table_words[:].bitcast(U32).indirect(two_sb[:]))
 
         y = [keep.tile([P, S], F32, name="y%d" % t) for t in range(PACK)]
         gate = [keep.tile([P, W], F32, name="gate%d" % t) for t in range(PACK)]
-        z_bf = keep.tile([P, S, PACK], BF16, name="z_bf", tag="z_bf_then_w2", align_bytes=64)
+        z_pairs = keep.tile([P, 2, S, 2], BF16, name="z_pairs")
+        z_bf = [keep.tile([P, S // 2, PACK], BF16, name="z_bf%d" % half, tag="z_bf%d" % half, align_bytes=64) for half in range(2)]
 
         def gates(t):
             for half in range(2):
                 nc.scalar.activation(gate[t][:, 192 * half : 192 * (half + 1)],
                                      y[t][:].indirect(n2_sb[:, 12 * half : 12 * (half + 1)]), ACT.Sigmoid)
 
-        def make_z(t, cols):
-            nc.vector.tensor_scalar(z_bf[:, cols, t], y[t][:, cols], gain[t][:], None, ALU.mult)
+        def make_z(t):
+            nc.vector.tensor_scalar(z_pairs[:, t // 2, :, t % 2], y[t][:], gain[t][:], None, ALU.mult)
 
         def interleave(copy, dst, src):
             copy(dst.rearrange("p (c i) j -> p c j i", i=4), src.rearrange("p j (c i) -> p c j i", i=4))
@@ -126,34 +128,38 @@ def tile_picked_mixinkgatelift_none_p_kernel(tc, x_words, x_scales, w1, gn, w2, 
                                 xb_words[:].bitcast(FP8X4), xb_scales[:], start=True, stop=False)
             h_ps.append(bank)
 
-        ra = [keep.tile([P, W], F32, name="ra%d" % t, tag="slot%d" % t, align_bytes=64) for t in range(2)]
-        old = keep.tile([P, 2, W], F32, name="old")
+        by_vector = keep.tile([P, 3, W], F32, name="by_vector", tag="slot1", align_bytes=64)
+        by_scalar = keep.tile([P, W], F32, name="by_scalar")
+        fetched = [by_vector[:, 0, :], by_vector[:, 1, :], by_scalar[:], by_vector[:, 2, :]]
         for t in range(PACK):
             nc.scalar.copy(y[t][:], y_ps[t][:])
             gates(t)
             if t < 2:
-                nc.vector.tensor_tensor(ra[t][:], y[t][:].indirect(n1_sb[:]), gate[t][:], ALU.mult)
+                nc.vector.tensor_tensor(fetched[t], y[t][:].indirect(n1_sb[:]), gate[t][:], ALU.mult)
+            elif t == 2:
+                nc.scalar.activation(fetched[t], y[t][:].indirect(n1_sb[:]), ACT.Copy)
             else:
-                nc.scalar.activation(old[:, t - 2, :], y[t][:].indirect(n1_sb[:]), ACT.Copy)
-                nc.vector.tensor_tensor(y[t][:].indirect(n1_sb[:]), old[:, t - 2, :], gate[t][:], ALU.mult)
+                nc.vector.tensor_copy(fetched[t], y[t][:].indirect(n1_sb[:]))
+        for t in (2, 3):
+            nc.vector.tensor_tensor(y[t][:].indirect(n1_sb[:]), fetched[t], gate[t][:], ALU.mult)
         for t in (0, 1):
-            nc.scalar.activation(y[t][:].indirect(n1_sb[:]), ra[t][:], ACT.Copy)
-        for t in (2, 3, 0):
-            make_z(t, slice(0, S))
-        halves = [slice(0, S // 2), slice(S // 2, S)]
-        for cols in halves:
-            make_z(1, cols)
+            nc.scalar.activation(y[t][:].indirect(n1_sb[:]), fetched[t], ACT.Copy)
+        for t in (2, 3, 0, 1):
+            make_z(t)
+        for half in range(2):
+            nc.vector.tensor_copy(z_bf[half][:].bitcast(F32),
+                                  z_pairs[:].bitcast(F32).rearrange("p a s o -> p s (a o)")[:, halves[half], :])
 
         w2_bf = keep.tile([P, N, PACK], BF16, name="w2_bf", tag="slot1", align_bytes=64)
         for u in range(4):
             cols = slice(P * u, P * (u + 1))
             interleave(nc.scalar.copy, w2_bf[:, cols, :], w2_raw[:, :, cols])
         z_words, z_scales = mx_tiles("z", S)
-        for cols in halves:
-            nc.vector.quantize_mx(z_words[:, cols].bitcast(FP8X4), z_scales[:, cols],
-                                  z_bf[:, cols, :].rearrange("p s t -> p (s t)"))
+        for half in range(2):
+            nc.vector.quantize_mx(z_words[:, halves[half]].bitcast(FP8X4), z_scales[:, halves[half]],
+                                  z_bf[half][:].rearrange("p s t -> p (s t)"))
         w2_first = keep.tile([P, P], U32, name="w2_first", align_bytes=64)
-        w2_rest = keep.tile([P, 3, P], U32, name="w2_rest", tag="z_bf_then_w2", align_bytes=64)
+        w2_rest = keep.tile([P, 3, P], U32, name="w2_rest", tag="z_bf1", align_bytes=64)
         w2_scales = keep.tile([P, N], U8, name="w2_scales", align_bytes=64)
         for u in range(4):
             cols = slice(P * u, P * (u + 1))

@@ -31,13 +31,12 @@ def tile_picked_mixinkgatelift_none_p_kernel(tc, x_words, x_scales, w1, gn, w2, 
             nc.sync.dma_start(dst[:], src)
             return dst
 
+        table_scales = keep.tile([P, T], U8, name="table_scales")
+        nc.gpsimd.memset(table_scales[:].bitcast(I32), 0)
         warm_in = keep.tile([P, 1], F32, name="warm_in")
         warm_out = keep.tile([P, 1], F32, name="warm_out")
-        nc.gpsimd.memset(warm_in[:], 0.0)
+        nc.vector.memset(warm_in[:], 0.0)
         nc.scalar.activation(warm_out[:], warm_in[:], ACT.Sigmoid)
-
-        table_scales = keep.tile([P, T], U8, name="table_scales")
-        nc.vector.memset(table_scales[:].bitcast(I32), 0)
         offs_sb = load_list(offs, "offs_sb")
         two_sb = load_list(two, "two_sb")
         for q in range(4):
@@ -130,21 +129,21 @@ def tile_picked_mixinkgatelift_none_p_kernel(tc, x_words, x_scales, w1, gn, w2, 
 
         by_vector = keep.tile([P, 3, W], F32, name="by_vector", tag="slot1", align_bytes=64)
         by_scalar = keep.tile([P, W], F32, name="by_scalar")
-        fetched = [by_vector[:, 0, :], by_vector[:, 1, :], by_scalar[:], by_vector[:, 2, :]]
+        fetched = [by_vector[:, 0, :], by_vector[:, 1, :], by_vector[:, 2, :], by_scalar[:]]
         for t in range(PACK):
             nc.scalar.copy(y[t][:], y_ps[t][:])
             gates(t)
-            if t < 2:
+            if t % 2 == 0:
                 nc.vector.tensor_tensor(fetched[t], y[t][:].indirect(n1_sb[:]), gate[t][:], ALU.mult)
-            elif t == 2:
-                nc.scalar.activation(fetched[t], y[t][:].indirect(n1_sb[:]), ACT.Copy)
             else:
-                nc.vector.tensor_copy(fetched[t], y[t][:].indirect(n1_sb[:]))
-        for t in (2, 3):
-            nc.vector.tensor_tensor(y[t][:].indirect(n1_sb[:]), fetched[t], gate[t][:], ALU.mult)
-        for t in (0, 1):
+                if t == 1:
+                    nc.vector.tensor_copy(fetched[t], y[t][:].indirect(n1_sb[:]))
+                else:
+                    nc.scalar.activation(fetched[t], y[t][:].indirect(n1_sb[:]), ACT.Copy)
+                nc.vector.tensor_tensor(y[t][:].indirect(n1_sb[:]), fetched[t], gate[t][:], ALU.mult)
+        for t in (0, 2):
             nc.scalar.activation(y[t][:].indirect(n1_sb[:]), fetched[t], ACT.Copy)
-        for t in (2, 3, 0, 1):
+        for t in (1, 3, 0, 2):
             make_z(t)
         for half in range(2):
             nc.vector.tensor_copy(z_bf[half][:].bitcast(F32),
@@ -158,7 +157,7 @@ def tile_picked_mixinkgatelift_none_p_kernel(tc, x_words, x_scales, w1, gn, w2, 
         for half in range(2):
             nc.vector.quantize_mx(z_words[:, halves[half]].bitcast(FP8X4), z_scales[:, halves[half]],
                                   z_bf[half][:].rearrange("p s t -> p (s t)"))
-        w2_first = keep.tile([P, P], U32, name="w2_first", align_bytes=64)
+        w2_first = keep.tile([P, P], U32, name="w2_first", tag="z_bf0", align_bytes=64)
         w2_rest = keep.tile([P, 3, P], U32, name="w2_rest", tag="z_bf1", align_bytes=64)
         w2_scales = keep.tile([P, N], U8, name="w2_scales", align_bytes=64)
         for u in range(4):

from contextlib import ExitStack

import concourse.mybir as mybir

K, T, S, N, H, W, U = 512, 2048, 512, 512, 512, 384, 256
FLOPS = 2 * K * H * S + 2 * H * N * S + 2 * K * N * S

F32 = mybir.dt.float32
BF16 = mybir.dt.bfloat16
I32 = mybir.dt.int32
U32 = mybir.dt.uint32
U16 = mybir.dt.uint16
U8 = mybir.dt.uint8
FP8X4 = mybir.dt.float8_e4m3fn_x4
ALU = mybir.AluOpType
ACT = mybir.ActivationFunctionType

P = 128
PACK = 4
QUARTERS = 4


def tile_picked_mixinkgatelift_none_p_kernel(tc, x_words, x_scales, w1, gn, w2, w3, offs, n1, n2, two, n3, n4, out):
    nc = tc.nc
    with ExitStack() as ctx:
        keep = ctx.enter_context(tc.tile_pool(name="keep", bufs=1))
        psum = ctx.enter_context(tc.psum_pool(name="psum", bufs=1))

        def load_list(src, name):
            dst = keep.tile(list(src.shape), U16, name=name)
            nc.sync.dma_start(dst[:], src)
            return dst

        table_scales = keep.tile([P, T], U8, name="table_scales")
        nc.gpsimd.memset(table_scales[:].bitcast(I32), 0)
        warm_in = keep.tile([P, 1], F32, name="warm_in")
        warm_out = keep.tile([P, 1], F32, name="warm_out")
        nc.vector.memset(warm_in[:], 0.0)
        nc.scalar.activation(warm_out[:], warm_in[:], ACT.Sigmoid)
        offs_sb = load_list(offs, "offs_sb")
        two_sb = load_list(two, "two_sb")
        for q in range(4):
            nc.sync.dma_start(table_scales[32 * q : 32 * q + 4, :].bitcast(I32), x_scales[0, 4 * q : 4 * q + 4, :].bitcast(I32))
        w1_raw = keep.tile([P, PACK, H], F32, name="w1_raw")
        nc.sync.dma_start(w1_raw[:], w1.rearrange("(p j) c -> p j c", j=PACK))
        table_words = keep.tile([P, T], I32, name="table_words")
        nc.sync.dma_start(table_words[:], x_words[0].rearrange("p c r -> p (c r)").bitcast(I32))
        n2_sb = load_list(n2, "n2_sb")
        n1_sb = load_list(n1, "n1_sb")
        w3_rows = w3.rearrange("(p j) m -> p j m", j=PACK)
        w3_raw = []
        for half in range(2):
            part = keep.tile([P, PACK, N // 2], F32, name="w3_raw%d" % half, tag="slot%d" % half, align_bytes=64)
            nc.sync.dma_start(part[:], w3_rows[:, :, 256 * half : 256 * (half + 1)])
            w3_raw.append(part)
        w2_raw = keep.tile([P, PACK, N], F32, name="w2_raw")
        w2_rows = w2.rearrange("(b t e) m -> t b e m", t=PACK, e=8)
        for t in range(PACK):
            nc.sync.dma_start(w2_raw[:, t, :], w2_rows[t])
        gain_rows = gn.rearrange("(b t e) o -> t b e o", t=PACK, e=8)
        gain = [keep.tile([P, 1], F32, name="gain%d" % t) for t in range(PACK)]
        for t in range(PACK):
            nc.sync.dma_start(gain[t][:], gain_rows[t])
        n3_sb = load_list(n3, "n3_sb")
        n4_sb = load_list(n4, "n4_sb")

        def mx_tiles(name, width):
            return (keep.tile([P, width], U32, name=name + "_words", align_bytes=64),
                    keep.tile([P, width], U8, name=name + "_scales", align_bytes=64))

        xa_words, xa_scales = mx_tiles("xa", S)
        xb_words, xb_scales = mx_tiles("xb", S)
        halves = [slice(0, S // 2), slice(S // 2, S)]
        nc.vector.tensor_copy(xa_scales[:], table_scales[:].indirect(offs_sb[:]))
        nc.vector.tensor_copy(xb_scales[:], table_scales[:].indirect(two_sb[:]))

        w1_bf = keep.tile([P, PACK, 16, 8, PACK], BF16, name="w1_bf", align_bytes=64)
        dst = w1_bf[:].rearrange("p t b e j -> p b t e j")
        src = w1_raw[:].rearrange("p j (b t e) -> p b t e j", t=PACK, e=8)
        nc.scalar.copy(dst[:, :6], src[:, :6])
        nc.vector.tensor_copy(dst[:, 6:], src[:, 6:])
        w1_words, w1_scales = mx_tiles("w1", H)
        nc.vector.quantize_mx(w1_words[:].bitcast(FP8X4), w1_scales[:], w1_bf[:].rearrange("p t b e j -> p (t b e j)"))
        for half in range(2):
            nc.vector.tensor_copy(xa_words[:, halves[half]],
                                  table_words[:].bitcast(U32).indirect(offs_sb[:, 16 * half : 16 * (half + 1)]))
        nc.vector.tensor_copy(xb_words[:], table_words[:].bitcast(U32).indirect(two_sb[:]))
        y_ps = []
        for t in range(PACK):
            cols = slice(P * t, P * (t + 1))
            bank = psum.tile([P, S], F32, name="y_ps%d" % t)
            for part in halves:
                nc.tensor.matmul_mx(bank[:, part], w1_words[:, cols].bitcast(FP8X4), w1_scales[:, cols],
                                    xa_words[:, part].bitcast(FP8X4), xa_scales[:, part], start=True, stop=True)
            y_ps.append(bank)

        y = [keep.tile([P, S], F32, name="y%d" % t) for t in range(PACK)]
        gate = [keep.tile([P, W], F32, name="gate%d" % t) for t in range(PACK)]
        z_pairs = keep.tile([P, 2, S, 2], BF16, name="z_pairs")
        z_bf = [keep.tile([P, S // 2, PACK], BF16, name="z_bf%d" % half, tag="z_bf%d" % half, align_bytes=64) for half in range(2)]

        def gates(t):
            for half in range(2):
                nc.scalar.activation(gate[t][:, 192 * half : 192 * (half + 1)],
                                     y[t][:].indirect(n2_sb[:, 12 * half : 12 * (half + 1)]), ACT.Sigmoid)

        def make_z(t):
            nc.vector.tensor_scalar(z_pairs[:, t // 2, :, t % 2], y[t][:], gain[t][:], None, ALU.mult)

        def interleave(copy, dst, src):
            copy(dst.rearrange("p (c i) j -> p c j i", i=4), src.rearrange("p j (c i) -> p c j i", i=4))

        def quantise(name, src):
            words, scales = mx_tiles(name, N)
            nc.vector.quantize_mx(words[:].bitcast(FP8X4), scales[:], src[:].rearrange("p m j -> p (m j)"))
            return words, scales

        w3_bf = keep.tile([P, N, PACK], BF16, name="w3_bf", align_bytes=64)
        for half in range(2):
            interleave(nc.vector.tensor_copy, w3_bf[:, 256 * half : 256 * (half + 1), :], w3_raw[half][:])
        w3_words, w3_scales = quantise("w3", w3_bf)
        h_ps = []
        for u in range(4):
            cols = slice(P * u, P * (u + 1))
            bank = psum.tile([P, S], F32, name="h_ps%d" % u)
            nc.tensor.matmul_mx(bank[:], w3_words[:, cols].bitcast(FP8X4), w3_scales[:, cols],
                                xb_words[:].bitcast(FP8X4), xb_scales[:], start=True, stop=False)
            h_ps.append(bank)

        by_vector = keep.tile([P, 3, W], F32, name="by_vector", tag="slot1", align_bytes=64)
        by_scalar = keep.tile([P, W], F32, name="by_scalar")
        fetched = [by_vector[:, 0, :], by_vector[:, 1, :], by_vector[:, 2, :], by_scalar[:]]
        for t in range(PACK):
            nc.scalar.copy(y[t][:], y_ps[t][:])
            gates(t)
            if t % 2 == 0:
                nc.vector.tensor_tensor(fetched[t], y[t][:].indirect(n1_sb[:]), gate[t][:], ALU.mult)
            else:
                if t == 1:
                    nc.vector.tensor_copy(fetched[t], y[t][:].indirect(n1_sb[:]))
                else:
                    nc.scalar.activation(fetched[t], y[t][:].indirect(n1_sb[:]), ACT.Copy)
                nc.vector.tensor_tensor(y[t][:].indirect(n1_sb[:]), fetched[t], gate[t][:], ALU.mult)
        for t in (0, 2):
            nc.scalar.activation(y[t][:].indirect(n1_sb[:]), fetched[t], ACT.Copy)
        for t in (1, 3, 0, 2):
            make_z(t)
        for half in range(2):
            nc.vector.tensor_copy(z_bf[half][:].bitcast(F32),
                                  z_pairs[:].bitcast(F32).rearrange("p a s o -> p s (a o)")[:, halves[half], :])

        w2_bf = keep.tile([P, N, PACK], BF16, name="w2_bf", tag="slot1", align_bytes=64)
        for u in range(4):
            cols = slice(P * u, P * (u + 1))
            interleave(nc.scalar.copy, w2_bf[:, cols, :], w2_raw[:, :, cols])
        z_words, z_scales = mx_tiles("z", S)
        for half in range(2):
            nc.vector.quantize_mx(z_words[:, halves[half]].bitcast(FP8X4), z_scales[:, halves[half]],
                                  z_bf[half][:].rearrange("p s t -> p (s t)"))
        w2_first = keep.tile([P, P], U32, name="w2_first", tag="z_bf0", align_bytes=64)
        w2_rest = keep.tile([P, 3, P], U32, name="w2_rest", tag="z_bf1", align_bytes=64)
        w2_scales = keep.tile([P, N], U8, name="w2_scales", align_bytes=64)
        for u in range(4):
            cols = slice(P * u, P * (u + 1))
            words = w2_first[:] if u == 0 else w2_rest[:, u - 1, :]
            nc.vector.quantize_mx(words.bitcast(FP8X4), w2_scales[:, cols],
                                  w2_bf[:, cols, :].rearrange("p m j -> p (m j)"))
            for part in (halves if u == 0 else [slice(0, S)]):
                nc.tensor.matmul_mx(h_ps[u][:, part], words.bitcast(FP8X4), w2_scales[:, cols],
                                    z_words[:, part].bitcast(FP8X4), z_scales[:, part], start=False, stop=part.stop == S)

        h = [keep.tile([P, S], F32, name="h%d" % u) for u in range(4)]
        minus_pa = [keep.tile([P, U], F32, name="minus_pa%d" % u) for u in range(4)]
        pb = [keep.tile([P, U], F32, name="pb%d" % u) for u in range(4)]
        rb = [keep.tile([P, U], F32, name="rb%d" % u) for u in range(4)]
        res = [keep.tile([P, S], F32, name="res%d" % u) for u in range(4)]

        def fetch_pa(u):
            nc.scalar.activation(minus_pa[u][:], h[u][:].indirect(n3_sb[:]), ACT.Copy, scale=-1.0)

        def fetch_pb(u):
            if u == 3:
                nc.scalar.activation(pb[u][:], h[u][:].indirect(n4_sb[:]), ACT.Copy)
            else:
                nc.vector.tensor_copy(pb[u][:], h[u][:].indirect(n4_sb[:]))

        def larger(u):
            nc.vector.scalar_tensor_tensor(rb[u][:], minus_pa[u][:], -0.5, pb[u][:], ALU.mult, ALU.max)

        def put_difference(u):
            nc.vector.tensor_tensor(res[u][:].indirect(n3_sb[:]), pb[u][:], minus_pa[u][:], ALU.add)

        def put_larger(u):
            nc.scalar.activation(res[u][:].indirect(n4_sb[:]), rb[u][:], ACT.Copy)

        def store(u, queue):
            queue.dma_start(out[P * u : P * (u + 1), :], res[u][:])

        for u in range(4):
            (nc.vector.tensor_copy if u % 2 else nc.scalar.copy)(h[u][:], h_ps[u][:])
        for u in range(4):
            fetch_pa(u)
            fetch_pb(u)
            larger(u)
        for u in (0, 2):
            put_difference(u)
            put_larger(u + 1)
            put_larger(u)
            put_difference(u + 1)
            store(u, nc.sync if u == 0 else nc.scalar)
            store(u + 1, nc.sync)
